import numpy as np, ml_dtypes
CORES = [61,69,101,62,70,102]
N = 6
F = 256
GROUPS = [[0,3],[1,4],[2,5]]
def setup_inputs(rng):
    return {"x": rng.standard_normal((N, 128, F), dtype=np.float32).astype(ml_dtypes.bfloat16), "w": (rng.standard_normal((N, 128, 128), dtype=np.float32) / 11).astype(ml_dtypes.bfloat16)}
def setup_inputs_big(rng):
    d = setup_inputs(rng)
    for k in ("x", "w"): d[k] = (d[k].astype(np.float32) * 1024.0).astype(d[k].dtype)
    return d
def setup_inputs_small(rng):
    d = setup_inputs(rng)
    for k in ("x", "w"): d[k] = (d[k].astype(np.float32) * (1 / 1024.0)).astype(d[k].dtype)
    return d
def setup_inputs_apart(rng):
    d = setup_inputs(rng)
    f = (10.0 ** rng.permutation(np.linspace(-1.5, 1.5, N))).astype(np.float32).reshape(N, 1, 1)
    for k in ("x", "w"): d[k] = (d[k].astype(np.float32) * f).astype(d[k].dtype)
    return d
def reference(x, w):
    X, W = x.astype(np.float64), w.astype(np.float64)
    s = sum(W[g[0]].T @ np.maximum(sum(X[j] for j in g), 0.0) for g in GROUPS).astype(ml_dtypes.bfloat16)
    return {"y": np.broadcast_to(s, (N,) + s.shape)}

@@ -1,0 +1,127 @@
+from concourse.bass import DstId, RemoteDMATransfer
+from concourse.mybir import AluOpType
+
+F = 256
+K = 128
+H = F // 2
+NG = 3
+
+SCRATCH = {
+    "xw":   ("sbuf", [128, F + K], "bfloat16"),
+    "land": ("sbuf", [128, F + K], "bfloat16"),
+    "zero": ("sbuf", [128, F], "bfloat16"),
+    "m":    ("sbuf", [128, F], "bfloat16"),
+    "pown": ("sbuf", [128, F], "bfloat16"),
+    "yout": ("sbuf", [128, F], "bfloat16"),
+    "na":   ("psum", [128, 512], "float32"),
+    "acc0": ("psum", [128, 512], "float32"),
+    "acc1": ("psum", [128, 512], "float32"),
+    "part": ("psum", [128, 512], "float32"),
+}
+SEMAPHORES = ["ld", "xin", "sent", "vz", "vn", "vm0", "vm1", "mm0", "mm1", "cp", "vs", "vy", "st"]
+for _s in range(NG):
+    SCRATCH["pl%d" % _s] = ("sbuf", [128, F], "bfloat16")
+    SEMAPHORES.append("pa%d" % _s)
+
+
+def _engines(core, T, topo):
+    eng = None
+    for c in T.cores:
+        if c != core:
+            eng = topo.mask(core, c) if eng is None else eng & topo.mask(core, c)
+    return eng
+
+
+def _count(mask):
+    return bin(mask).count("1")
+
+
+def _plan(T, topo):
+    groups = [[T.cores[r] for r in grp] for grp in T.tables["GROUPS"]]
+    sender = {}
+    for s, gs in enumerate(groups):
+        load = {m: 0 for m in gs}
+        dests = [d for d in range(len(groups)) if d != s]
+        ok = {d: [m for m in gs if all(topo.may_write(m, c) for c in groups[d])] for d in dests}
+        for d in sorted(dests, key=lambda d: len(ok[d])):
+            m = min(ok[d], key=lambda c: load[c])
+            load[m] += len(groups[d])
+            sender[(s, d)] = m
+    return groups, sender
+
+
+def rank_program(g, core, T, topo):
+    if T.rank_of(core) is None:
+        return
+    S = T.sem
+    groups, sender = _plan(T, topo)
+    gi = [i for i, grp in enumerate(groups) if core in grp][0]
+    grp = groups[gi]
+    partner = [c for c in grp if c != core][0]
+    first = core == grp[0]
+    writes = {c: sum(len(groups[p[1]]) for p in sender if sender[p] == c) for c in T.cores}
+    dests = [c for p in sorted(sender) if sender[p] == core for c in groups[p[1]]]
+    srcs = sorted([s for s in range(len(groups)) if s != gi], key=lambda s: writes[sender[(s, gi)]])
+    eng = _engines(core, T, topo)
+    n = _count(eng)
+    from_partner = _count(_engines(partner, T, topo))
+    loads = 32 if first else 16
+
+    W = T.xw[:, F:F + K] if first else T.land[:, F:F + K]
+    acc = [T.acc0, T.acc1]
+    vm = [S.vm0, S.vm1]
+    mm = [S.mm0, S.mm1]
+    blocks = [(0, H), (H, F)]
+
+    g.sync.dma_start(T.xw[:, 0:F], T.x[:]).then_inc(S.ld, 16)
+    if first:
+        g.scalar.dma_start(T.xw[:, F:F + K], T.w[:]).then_inc(S.ld, 16)
+
+    g.wait_ge(S.ld, loads)
+    width = F + K if first else F
+    rid, pid, _ = topo.addr(partner)
+    g.remote_dma(T.land[:, 0:width], T.xw[:, 0:width], S.xin, S.sent, pid, rid, eng)
+    sent = n
+    if dests:
+        g.wait_ge(S.cp, 2)
+        ids = [DstId(rid=topo.addr(c)[0], pnc=topo.addr(c)[1]) for c in dests]
+        g.remote_dma_fused([RemoteDMATransfer(dst_ids=ids, dma_engine_mask=eng, remote_sem=S["pa%d" % gi],
+                                              srcs=[T.pown[:]], dsts=[T["pl%d" % gi][:] for c in dests], alu_op=0)],
+                           local_sem=S.sent)
+        sent += n
+    g.wait_ge(S.sent, sent)
+
+    te = g.tensor
+    te.wait_ge(S.ld, loads)
+    if not first:
+        te.wait_ge(S.xin, from_partner)
+    for k, (lo, hi) in enumerate(blocks):
+        te.matmul(acc[k][:, 0:H], W, T.xw[:, lo:hi], True, False)
+    for k, (lo, hi) in enumerate(blocks):
+        te.wait_ge(vm[k], 1)
+        te.matmul(acc[k][:, 0:H], W, T.m[:, lo:hi], False, True).then_inc(mm[k], 1)
+
+    v = g.vector
+    v.memset(T.zero[:], 0.0).then_inc(S.vz, 1)
+    v.wait_ge(S.ld, loads)
+    v.wait_ge(S.vz, 1)
+    v.tensor_tensor(T.na[:, 0:F], T.zero[:], T.xw[:, 0:F], AluOpType.subtract).then_inc(S.vn, 1)
+    v.wait_ge(S.vn, 1)
+    v.wait_ge(S.xin, from_partner)
+    for k, (lo, hi) in enumerate(blocks):
+        v.tensor_tensor(T.m[:, lo:hi], T.na[:, lo:hi], T.land[:, lo:hi], AluOpType.max).then_inc(vm[k], 1)
+    for k, (lo, hi) in enumerate(blocks):
+        v.wait_ge(mm[k], 1)
+        if dests:
+            v.tensor_copy(T.pown[:, lo:hi], acc[k][:, 0:H]).then_inc(S.cp, 1)
+    early, late = srcs
+    v.wait_ge(S["pa%d" % early], _count(_engines(sender[(early, gi)], T, topo)))
+    for k, (lo, hi) in enumerate(blocks):
+        v.tensor_tensor(T.part[:, lo:hi], acc[k][:, 0:H], T["pl%d" % early][:, lo:hi], AluOpType.add).then_inc(S.vs, 1)
+    v.wait_ge(S.vs, 2)
+    v.wait_ge(S["pa%d" % late], _count(_engines(sender[(late, gi)], T, topo)))
+    v.tensor_tensor(T.yout[:], T.part[:, 0:F], T["pl%d" % late][:], AluOpType.add).then_inc(S.vy, 1)
+
+    g.sync.wait_ge(S.vy, 1)
+    g.sync.dma_start(T.y[:], T.yout[:]).then_inc(S.st, 16)
+    g.sync.wait_ge(S.st, 16)

@@ -12,23 +12,23 @@ SCRATCH = {
     "zero": ("sbuf", [128, F], "bfloat16"),
     "m":    ("sbuf", [128, F], "bfloat16"),
     "pown": ("sbuf", [128, F], "bfloat16"),
+    "q":    ("sbuf", [128, F], "bfloat16"),
     "yout": ("sbuf", [128, F], "bfloat16"),
     "na":   ("psum", [128, 512], "float32"),
     "acc0": ("psum", [128, 512], "float32"),
     "acc1": ("psum", [128, 512], "float32"),
     "part": ("psum", [128, 512], "float32"),
 }
-SEMAPHORES = ["ld", "xin", "sent", "vz", "vn", "vm0", "vm1", "mm0", "mm1", "cp", "vs", "vy", "st"]
+SEMAPHORES = ["ld", "xin", "sent", "yin", "vz", "vn", "vm0", "vm1", "mm0", "mm1", "cp", "vq", "vs", "vy", "st"]
 for _s in range(NG):
     SCRATCH["pl%d" % _s] = ("sbuf", [128, F], "bfloat16")
     SEMAPHORES.append("pa%d" % _s)
 
 
-def _engines(core, T, topo):
+def _common(core, dests, topo):
     eng = None
-    for c in T.cores:
-        if c != core:
-            eng = topo.mask(core, c) if eng is None else eng & topo.mask(core, c)
+    for c in dests:
+        eng = topo.mask(core, c) if eng is None else eng & topo.mask(core, c)
     return eng
 
 
@@ -42,10 +42,10 @@ def _plan(T, topo):
     for s, gs in enumerate(groups):
         load = {m: 0 for m in gs}
         dests = [d for d in range(len(groups)) if d != s]
-        ok = {d: [m for m in gs if all(topo.may_write(m, c) for c in groups[d])] for d in dests}
+        ok = {d: [m for m in gs if topo.may_write(m, groups[d][0])] for d in dests}
         for d in sorted(dests, key=lambda d: len(ok[d])):
             m = min(ok[d], key=lambda c: load[c])
-            load[m] += len(groups[d])
+            load[m] += 1
             sender[(s, d)] = m
     return groups, sender
 
@@ -59,12 +59,18 @@ def rank_program(g, core, T, topo):
     grp = groups[gi]
     partner = [c for c in grp if c != core][0]
     first = core == grp[0]
-    writes = {c: sum(len(groups[p[1]]) for p in sender if sender[p] == c) for c in T.cores}
-    dests = [c for p in sorted(sender) if sender[p] == core for c in groups[p[1]]]
-    srcs = sorted([s for s in range(len(groups)) if s != gi], key=lambda s: writes[sender[(s, gi)]])
-    eng = _engines(core, T, topo)
-    n = _count(eng)
-    from_partner = _count(_engines(partner, T, topo))
+
+    def targets(c):
+        return [groups[p[1]][0] for p in sorted(sender) if sender[p] == c]
+
+    def lands(s):
+        c = sender[(s, gi)]
+        return _count(_common(c, targets(c), topo))
+
+    dests = targets(core)
+    early, late = sorted([s for s in range(len(groups)) if s != gi], key=lambda s: len(targets(sender[(s, gi)])))
+    on = topo.mask(core, partner)
+    from_partner = _count(topo.mask(partner, core))
     loads = 32 if first else 16
 
     W = T.xw[:, F:F + K] if first else T.land[:, F:F + K]
@@ -80,15 +86,23 @@ def rank_program(g, core, T, topo):
     g.wait_ge(S.ld, loads)
     width = F + K if first else F
     rid, pid, _ = topo.addr(partner)
-    g.remote_dma(T.land[:, 0:width], T.xw[:, 0:width], S.xin, S.sent, pid, rid, eng)
-    sent = n
+    g.remote_dma(T.land[:, 0:width], T.xw[:, 0:width], S.xin, S.sent, pid, rid, on)
+    sent = _count(on)
     if dests:
+        off = _common(core, dests, topo)
         g.wait_ge(S.cp, 2)
         ids = [DstId(rid=topo.addr(c)[0], pnc=topo.addr(c)[1]) for c in dests]
-        g.remote_dma_fused([RemoteDMATransfer(dst_ids=ids, dma_engine_mask=eng, remote_sem=S["pa%d" % gi],
+        g.remote_dma_fused([RemoteDMATransfer(dst_ids=ids, dma_engine_mask=off, remote_sem=S["pa%d" % gi],
                                               srcs=[T.pown[:]], dsts=[T["pl%d" % gi][:] for c in dests], alu_op=0)],
                            local_sem=S.sent)
-        sent += n
+        sent += _count(off)
+    if first:
+        g.wait_ge(S.vq, 2)
+        g.wait_ge(S["pa%d" % late], lands(late))
+        g.remote_dma_fused([RemoteDMATransfer(dst_ids=[DstId(rid=rid, pnc=pid)], dma_engine_mask=on, remote_sem=S.yin,
+                                              srcs=[T.q[:], T["pl%d" % late][:]], dsts=[T.yout[:]], alu_op=1)],
+                           local_sem=S.sent)
+        sent += _count(on)
     g.wait_ge(S.sent, sent)
 
     te = g.tensor
@@ -114,14 +128,19 @@ def rank_program(g, core, T, topo):
         v.wait_ge(mm[k], 1)
         if dests:
             v.tensor_copy(T.pown[:, lo:hi], acc[k][:, 0:H]).then_inc(S.cp, 1)
-    early, late = srcs
-    v.wait_ge(S["pa%d" % early], _count(_engines(sender[(early, gi)], T, topo)))
-    for k, (lo, hi) in enumerate(blocks):
-        v.tensor_tensor(T.part[:, lo:hi], acc[k][:, 0:H], T["pl%d" % early][:, lo:hi], AluOpType.add).then_inc(S.vs, 1)
-    v.wait_ge(S.vs, 2)
-    v.wait_ge(S["pa%d" % late], _count(_engines(sender[(late, gi)], T, topo)))
-    v.tensor_tensor(T.yout[:], T.part[:, 0:F], T["pl%d" % late][:], AluOpType.add).then_inc(S.vy, 1)
+    if first:
+        v.wait_ge(S["pa%d" % early], lands(early))
+        for k, (lo, hi) in enumerate(blocks):
+            v.tensor_tensor(T.q[:, lo:hi], acc[k][:, 0:H], T["pl%d" % early][:, lo:hi], AluOpType.add).then_inc(S.vq, 1)
+        for k, (lo, hi) in enumerate(blocks):
+            v.tensor_tensor(T.part[:, lo:hi], acc[k][:, 0:H], T["pl%d" % early][:, lo:hi], AluOpType.add).then_inc(S.vs, 1)
+        v.wait_ge(S.vs, 2)
+        v.wait_ge(S["pa%d" % late], lands(late))
+        v.tensor_tensor(T.yout[:], T.part[:, 0:F], T["pl%d" % late][:], AluOpType.add).then_inc(S.vy, 1)
 
-    g.sync.wait_ge(S.vy, 1)
+    if first:
+        g.sync.wait_ge(S.vy, 1)
+    else:
+        g.sync.wait_ge(S.yin, from_partner)
     g.sync.dma_start(T.y[:], T.yout[:]).then_inc(S.st, 16)
     g.sync.wait_ge(S.st, 16)

from concourse.bass import DstId, RemoteDMATransfer
from concourse.mybir import AluOpType

F = 256
K = 128
H = F // 2
NG = 3

SCRATCH = {
    "xw":   ("sbuf", [128, F + K], "bfloat16"),
    "land": ("sbuf", [128, F + K], "bfloat16"),
    "zero": ("sbuf", [128, F], "bfloat16"),
    "m":    ("sbuf", [128, F], "bfloat16"),
    "pown": ("sbuf", [128, F], "bfloat16"),
    "q":    ("sbuf", [128, F], "bfloat16"),
    "yout": ("sbuf", [128, F], "bfloat16"),
    "na":   ("psum", [128, 512], "float32"),
    "acc0": ("psum", [128, 512], "float32"),
    "acc1": ("psum", [128, 512], "float32"),
    "part": ("psum", [128, 512], "float32"),
}
SEMAPHORES = ["ld", "xin", "sent", "yin", "vz", "vn", "vm0", "vm1", "mm0", "mm1", "cp", "vq", "vs", "vy", "st"]
for _s in range(NG):
    SCRATCH["pl%d" % _s] = ("sbuf", [128, F], "bfloat16")
    SEMAPHORES.append("pa%d" % _s)


def _common(core, dests, topo):
    eng = None
    for c in dests:
        eng = topo.mask(core, c) if eng is None else eng & topo.mask(core, c)
    return eng


def _count(mask):
    return bin(mask).count("1")


def _plan(T, topo):
    groups = [[T.cores[r] for r in grp] for grp in T.tables["GROUPS"]]
    sender = {}
    for s, gs in enumerate(groups):
        load = {m: 0 for m in gs}
        dests = [d for d in range(len(groups)) if d != s]
        ok = {d: [m for m in gs if topo.may_write(m, groups[d][0])] for d in dests}
        for d in sorted(dests, key=lambda d: len(ok[d])):
            m = min(ok[d], key=lambda c: load[c])
            load[m] += 1
            sender[(s, d)] = m
    return groups, sender


def rank_program(g, core, T, topo):
    if T.rank_of(core) is None:
        return
    S = T.sem
    groups, sender = _plan(T, topo)
    gi = [i for i, grp in enumerate(groups) if core in grp][0]
    grp = groups[gi]
    partner = [c for c in grp if c != core][0]
    first = core == grp[0]

    def targets(c):
        return [groups[p[1]][0] for p in sorted(sender) if sender[p] == c]

    def lands(s):
        c = sender[(s, gi)]
        return _count(_common(c, targets(c), topo))

    dests = targets(core)
    early, late = sorted([s for s in range(len(groups)) if s != gi], key=lambda s: len(targets(sender[(s, gi)])))
    on = topo.mask(core, partner)
    from_partner = _count(topo.mask(partner, core))
    loads = 32 if first else 16

    W = T.xw[:, F:F + K] if first else T.land[:, F:F + K]
    acc = [T.acc0, T.acc1]
    vm = [S.vm0, S.vm1]
    mm = [S.mm0, S.mm1]
    blocks = [(0, H), (H, F)]

    g.sync.dma_start(T.xw[:, 0:F], T.x[:]).then_inc(S.ld, 16)
    if first:
        g.scalar.dma_start(T.xw[:, F:F + K], T.w[:]).then_inc(S.ld, 16)

    g.wait_ge(S.ld, loads)
    width = F + K if first else F
    rid, pid, _ = topo.addr(partner)
    g.remote_dma(T.land[:, 0:width], T.xw[:, 0:width], S.xin, S.sent, pid, rid, on)
    sent = _count(on)
    if dests:
        off = _common(core, dests, topo)
        g.wait_ge(S.cp, 2)
        ids = [DstId(rid=topo.addr(c)[0], pnc=topo.addr(c)[1]) for c in dests]
        g.remote_dma_fused([RemoteDMATransfer(dst_ids=ids, dma_engine_mask=off, remote_sem=S["pa%d" % gi],
                                              srcs=[T.pown[:]], dsts=[T["pl%d" % gi][:] for c in dests], alu_op=0)],
                           local_sem=S.sent)
        sent += _count(off)
    if first:
        g.wait_ge(S.vq, 2)
        g.wait_ge(S["pa%d" % late], lands(late))
        g.remote_dma_fused([RemoteDMATransfer(dst_ids=[DstId(rid=rid, pnc=pid)], dma_engine_mask=on, remote_sem=S.yin,
                                              srcs=[T.q[:], T["pl%d" % late][:]], dsts=[T.yout[:]], alu_op=1)],
                           local_sem=S.sent)
        sent += _count(on)
    g.wait_ge(S.sent, sent)

    te = g.tensor
    te.wait_ge(S.ld, loads)
    if not first:
        te.wait_ge(S.xin, from_partner)
    for k, (lo, hi) in enumerate(blocks):
        te.matmul(acc[k][:, 0:H], W, T.xw[:, lo:hi], True, False)
    for k, (lo, hi) in enumerate(blocks):
        te.wait_ge(vm[k], 1)
        te.matmul(acc[k][:, 0:H], W, T.m[:, lo:hi], False, True).then_inc(mm[k], 1)

    v = g.vector
    v.memset(T.zero[:], 0.0).then_inc(S.vz, 1)
    v.wait_ge(S.ld, loads)
    v.wait_ge(S.vz, 1)
    v.tensor_tensor(T.na[:, 0:F], T.zero[:], T.xw[:, 0:F], AluOpType.subtract).then_inc(S.vn, 1)
    v.wait_ge(S.vn, 1)
    v.wait_ge(S.xin, from_partner)
    for k, (lo, hi) in enumerate(blocks):
        v.tensor_tensor(T.m[:, lo:hi], T.na[:, lo:hi], T.land[:, lo:hi], AluOpType.max).then_inc(vm[k], 1)
    for k, (lo, hi) in enumerate(blocks):
        v.wait_ge(mm[k], 1)
        if dests:
            v.tensor_copy(T.pown[:, lo:hi], acc[k][:, 0:H]).then_inc(S.cp, 1)
    if first:
        v.wait_ge(S["pa%d" % early], lands(early))
        for k, (lo, hi) in enumerate(blocks):
            v.tensor_tensor(T.q[:, lo:hi], acc[k][:, 0:H], T["pl%d" % early][:, lo:hi], AluOpType.add).then_inc(S.vq, 1)
        for k, (lo, hi) in enumerate(blocks):
            v.tensor_tensor(T.part[:, lo:hi], acc[k][:, 0:H], T["pl%d" % early][:, lo:hi], AluOpType.add).then_inc(S.vs, 1)
        v.wait_ge(S.vs, 2)
        v.wait_ge(S["pa%d" % late], lands(late))
        v.tensor_tensor(T.yout[:], T.part[:, 0:F], T["pl%d" % late][:], AluOpType.add).then_inc(S.vy, 1)

    if first:
        g.sync.wait_ge(S.vy, 1)
    else:
        g.sync.wait_ge(S.yin, from_partner)
    g.sync.dma_start(T.y[:], T.yout[:]).then_inc(S.st, 16)
    g.sync.wait_ge(S.st, 16)
